import numpy as np
import ml_dtypes


def mxq(x, axis, fmt="e4m3"):
    dtype, down = {"e4m3": (ml_dtypes.float8_e4m3fn, 7), "e5m2": (ml_dtypes.float8_e5m2, 14)}[fmt]
    v = np.moveaxis(np.asarray(x, np.float32).astype(ml_dtypes.bfloat16).astype(np.float64), axis, -1)
    blocks = v.reshape(v.shape[:-1] + (-1, 32))
    amax = np.abs(blocks).max(-1, keepdims=True)
    byte = np.maximum(np.where(amax > 0, np.frexp(amax)[1] - 1 + 127, 0) - down, 1)
    scale = np.exp2(byte - 127.0)
    codes = (blocks / scale).astype(np.float32).astype(dtype).astype(np.float64)
    return np.moveaxis((codes * scale).reshape(v.shape), -1, axis)


WIDE = False


def mx_kscale(k):
    if not WIDE:
        return np.ones(k)
    levels = np.array([10, -10, 5, -5, 0])
    if k % 512:
        return np.exp2(np.random.permutation(np.resize(levels, k // 32))).repeat(32)
    a = np.empty((k // 512, 16))
    for p in range(k // 512):
        a[p, :8] = np.random.permutation(np.resize(levels, 8))
        for g in range(8):
            far = levels[np.abs(levels - a[p, g]) >= 10]
            a[p, g + 8] = far[np.random.randint(len(far))]
    return np.exp2(a.ravel()).repeat(32)


def f64(x):
    return np.asarray(x).astype(np.float64)


def striped(idx):
    return np.tile(idx.reshape(-1, 16).T, (8, 1)).astype(np.uint16)


def unstriped(offs):
    return offs[:16].T.reshape(-1).astype(np.int64)


def pack_weight(w):
    k, n = w.shape
    w = f64(np.asarray(w, np.float32).astype(ml_dtypes.bfloat16)).reshape(k // 32, 32, n)
    amax = np.abs(w).max(1)
    byte = np.clip(np.where(amax > 0, np.frexp(amax)[1] - 1 + 127 - 7, 1), 1, 254)
    scaled = (w * np.exp2(127.0 - byte)[:, None, :]).reshape(k, n).astype(np.float32)
    words = np.ascontiguousarray(scaled.reshape(k // 512, 128, 4, n).transpose(0, 1, 3, 2)).astype(ml_dtypes.float8_e4m3fn).view(np.uint8)
    return words, np.ascontiguousarray(byte.astype(np.uint8).reshape(k // 512, 16, n))


def unpack_weight(words, scales):
    g, p, n, _ = words.shape
    vals = np.ascontiguousarray(words).view(ml_dtypes.float8_e4m3fn).astype(np.float64) * np.repeat(np.exp2(scales.astype(np.float64) - 127.0), 8, axis=1)[..., None]
    return vals.transpose(0, 1, 3, 2).reshape(g * 512, n)


E2M1 = np.array([0.0, 0.5, 1.0, 1.5, 2.0, 3.0, 4.0, 6.0, -0.0, -0.5, -1.0, -1.5, -2.0, -3.0, -4.0, -6.0])


def pack_fp4(w):
    k, n = w.shape
    w = f64(np.asarray(w, np.float32).astype(ml_dtypes.bfloat16)).reshape(k // 32, 32, n)
    amax = np.abs(w).max(1)
    mant, ex = np.frexp(amax / 6.0)
    byte = np.clip(np.where(amax > 0, np.where(mant > 0.5, ex, ex - 1) + 127, 1), 1, 254)
    scaled = (w * np.exp2(127.0 - byte)[:, None, :]).reshape(k, n).astype(np.float32)
    c = np.ascontiguousarray(scaled.reshape(k // 512, 128, 4, n).transpose(0, 1, 3, 2)).astype(ml_dtypes.float4_e2m1fn).view(np.uint8) & 0xF
    words = (c[..., 0::2] | (c[..., 1::2] << 4)).reshape(k // 512, 128, 2 * n)
    return np.ascontiguousarray(words), np.ascontiguousarray(byte.astype(np.uint8).reshape(k // 512, 16, n))


def unpack_fp4(words, scales):
    g, _, n = scales.shape
    words = np.ascontiguousarray(words).reshape(g, 128, n, 2)
    nib = np.empty((g, 128, n, 4), np.uint8)
    nib[..., 0::2] = words & 0xF
    nib[..., 1::2] = words >> 4
    vals = E2M1[nib] * np.repeat(np.exp2(scales.astype(np.float64) - 127.0), 8, axis=1)[..., None]
    return vals.transpose(0, 1, 3, 2).reshape(g * 512, n)


def relu(v):
    return np.maximum(v, 0.0)


K, T, S, H, N = 512, 1024, 512, 512, 256


def setup_inputs():
    n = np.random.standard_normal
    s = mx_kscale(K)[:, None]
    u = mx_kscale(H)
    packed_xT = pack_weight(n((K, T)) * s)
    packed_w2 = pack_fp4(n((H, N)) / np.sqrt(H) / u[:, None])
    return {
        "x_words": packed_xT[0],
        "x_scales": packed_xT[1],
        "w1": (n((K, H)) / np.sqrt(K) / s * u).astype(np.float32),
        "w2_words": packed_w2[0],
        "w2_scales": packed_w2[1],
        "offs": striped(np.random.permutation(T)[:S]),
    }


def reference(x_words, x_scales, w1, w2_words, w2_scales, offs):
    xq = unpack_weight(x_words, x_scales)[:, unstriped(offs)]
    h = relu(mxq(f64(w1), 0, "e4m3").T @ xq)
    z = h - h.mean(axis=1, keepdims=True)
    return unpack_fp4(w2_words, w2_scales).T @ mxq(z, 0, "e4m3")

@@ -1,0 +1,159 @@
+from contextlib import ExitStack
+
+import concourse.mybir as mybir
+
+K, T, S, H, N = 512, 1024, 512, 512, 256
+FLOPS = 2 * K * H * S + 2 * H * N * S
+
+F32 = mybir.dt.float32
+BF16 = mybir.dt.bfloat16
+I32 = mybir.dt.int32
+U32 = mybir.dt.uint32
+U16 = mybir.dt.uint16
+U8 = mybir.dt.uint8
+FP8X4 = mybir.dt.float8_e4m3fn_x4
+FP4X4 = mybir.dt.float4_e2m1fn_x4
+ALU = mybir.AluOpType
+ACT = mybir.ActivationFunctionType
+
+P = 128
+PACK = 4
+HALF = S // 2
+M_HALF = P // 2
+M_VECTOR = 44
+Z_VECTOR = 64
+
+
+def tile_picked_deepset_relu_p_kernel(tc, x_words, x_scales, w1, w2_words, w2_scales, offs, out):
+    nc = tc.nc
+    with ExitStack() as ctx:
+        sb = ctx.enter_context(tc.tile_pool(name="sb", bufs=1))
+        shared = ctx.enter_context(tc.tile_pool(name="shared", bufs=1))
+        ps = ctx.enter_context(tc.psum_pool(name="ps", bufs=1))
+
+        def tile(name, shape, dtype):
+            return sb.tile(shape, dtype, name=name, align_bytes=64)
+
+        offsets = tile("offsets", [P, S // 16], U16)
+        xs_all = tile("xs_all", [P, T], U8)
+        nc.vector.memset(xs_all[:].bitcast(I32), 0)
+        blank = shared.tile([P, 32], F32, name="blank", align_bytes=64, offset=4 * T - 64)
+        nc.vector.memset(blank[:], 0.0)
+        xw_all = shared.tile([P, T], U32, name="xw_all", align_bytes=64, offset=0)
+        seed = tile("seed", [P, 32], F32)
+        seed_out = tile("seed_out", [P, 1], F32)
+
+        nc.vector.tensor_copy(seed[:], blank[:])
+
+        w1_rows = w1.rearrange("(p j) c -> p j c", j=PACK)
+        w1_raw = [
+            tile("w1_raw0", [P, PACK, H // 2], F32),
+            shared.tile([P, PACK, H // 2], F32, name="w1_raw1", align_bytes=64, offset=4 * T),
+        ]
+
+        nc.sync.dma_start(w1_raw[0][:], w1_rows[:, :, 0:256])
+        nc.sync.dma_start(offsets[:], offs)
+        for q in range(4):
+            nc.sync.dma_start(xs_all[32 * q : 32 * q + 4, :].bitcast(I32), x_scales[0, 4 * q : 4 * q + 4, :].bitcast(I32))
+        nc.scalar.activation(seed_out[:], seed[:, 0:1], ACT.Relu)
+        nc.sync.dma_start(w1_raw[1][:], w1_rows[:, :, 256:512])
+        nc.sync.dma_start(xw_all[:].bitcast(I32), x_words[0].rearrange("p n t -> p (n t)").bitcast(I32))
+
+        xs = tile("xs", [P, S], U8)
+        nc.vector.tensor_copy(xs[:], xs_all[:].indirect(offsets[:]))
+
+        w1_bf = [tile("w1_bf%d" % h, [P, PACK, M_HALF, PACK], BF16) for h in range(2)]
+
+        def deal(copy, raw, raw_m0, half, m0, m1):
+            src = raw[:].rearrange("p j (m t) -> p m j t", t=PACK)[:, raw_m0 : raw_m0 + m1 - m0]
+            dst = w1_bf[half][:].rearrange("p t m j -> p m j t")[:, m0:m1]
+            copy(dst, src)
+
+        w1w = tile("w1w", [P, H], U32)
+        w1s = tile("w1s", [P, H], U8)
+
+        def quantize_w1(half):
+            for t in range(PACK):
+                cols = slice(P * t + M_HALF * half, P * t + M_HALF * (half + 1))
+                nc.vector.quantize_mx(w1w[:, cols].bitcast(FP8X4), w1s[:, cols], w1_bf[half][:, t].rearrange("p m j -> p (m j)"))
+
+        deal(nc.scalar.copy, w1_raw[0], 0, 0, 0, M_HALF)
+        deal(nc.vector.tensor_copy, w1_raw[1], 0, 1, 0, M_VECTOR)
+        quantize_w1(0)
+        deal(nc.scalar.copy, w1_raw[1], M_VECTOR, 1, M_VECTOR, M_HALF)
+        quantize_w1(1)
+
+        w2w = shared.tile([P, 2 * N], U8, name="w2w", align_bytes=64, offset=4 * T)
+        nc.sync.dma_start(w2w[:].bitcast(I32), w2_words[0].bitcast(I32))
+
+        w2s = shared.tile([P, N], U8, name="w2s", align_bytes=64, offset=4 * T + 2 * N)
+        nc.gpsimd.memset(w2s[:].bitcast(I32), 0)
+        for q in range(4):
+            nc.sync.dma_start(w2s[32 * q : 32 * q + 4, :].bitcast(I32), w2_scales[0, 4 * q : 4 * q + 4, :].bitcast(I32))
+        xw = [tile("xw%d" % h, [P, HALF], U32) for h in range(2)]
+        for h in range(2):
+            nc.vector.tensor_copy(xw[h][:], xw_all[:].indirect(offsets[:, 16 * h : 16 * (h + 1)]))
+
+        pre = [ps.tile([P, S], F32, name="pre%d" % t) for t in range(PACK)]
+
+        def layer1(t, h):
+            nc.tensor.matmul_mx(
+                pre[t][:, HALF * h : HALF * (h + 1)],
+                lhsT=w1w[:, P * t : P * (t + 1)].bitcast(FP8X4),
+                lhsT_scale=w1s[:, P * t : P * (t + 1)],
+                rhs=xw[h][:].bitcast(FP8X4),
+                rhs_scale=xs[:, HALF * h : HALF * (h + 1)],
+                start=True,
+                stop=True,
+            )
+
+        for t, h in ((0, 0), (1, 0), (0, 1), (1, 1), (2, 0), (2, 1), (3, 0), (3, 1)):
+            layer1(t, h)
+
+        hid = [tile("hid%d" % t, [P, S], F32) for t in range(PACK)]
+        total = [tile("total%d" % t, [P, 1], F32) for t in range(PACK)]
+        zt = tile("zt", [P, PACK, S], BF16)
+        for t in range(PACK):
+            if t == 1:
+                nc.vector.tensor_scalar(hid[t][:], pre[t][:], 0.0, None, ALU.max, ALU.add, accum_out=total[t][:])
+            else:
+                nc.scalar.activation(hid[t][:], pre[t][:], ACT.Relu, accum_out=total[t][:])
+        for t in range(PACK):
+            nc.vector.tensor_scalar(zt[:, t], hid[t][:], -float(S), total[t][:], ALU.mult, ALU.add)
+
+        zi = [tile("zi%d" % h, [P, HALF, PACK], BF16) for h in range(2)]
+
+        def weave(copy, h, c0, c1):
+            src = zt[:, :, HALF * h + c0 : HALF * h + c1].rearrange("p t (c i) -> p c t i", i=4)
+            dst = zi[h][:, c0:c1].rearrange("p (c i) t -> p c t i", i=4)
+            copy(dst, src)
+
+        weave(nc.vector.tensor_copy, 0, 0, HALF)
+        weave(nc.vector.tensor_copy, 1, 0, Z_VECTOR)
+        weave(nc.scalar.copy, 1, Z_VECTOR, HALF)
+
+        zw = [tile("zw%d" % h, [P, HALF], U32) for h in range(2)]
+        zs = [tile("zs%d" % h, [P, HALF], U8) for h in range(2)]
+        for h in range(2):
+            nc.vector.quantize_mx(zw[h][:].bitcast(FP8X4), zs[h][:], zi[h][:].rearrange("p c t -> p (c t)"))
+
+        for h in range(2):
+            for r in range(N // P):
+                acc = ps.tile([P, HALF], F32, name="acc%d%d" % (h, r))
+                nc.tensor.matmul_mx(
+                    acc[:],
+                    lhsT=w2w[:, 2 * P * r : 2 * P * (r + 1)].bitcast(FP4X4),
+                    lhsT_scale=w2s[:, P * r : P * (r + 1)],
+                    rhs=zw[h][:].bitcast(FP8X4),
+                    rhs_scale=zs[h][:],
+                    start=True,
+                    stop=True,
+                )
+                res = tile("res%d%d" % (h, r), [P, HALF], F32)
+                dst = out[P * r : P * (r + 1), HALF * h : HALF * (h + 1)]
+                if (h, r) == (1, 0):
+                    nc.vector.tensor_scalar(res[:], acc[:], -1.0 / S, None, ALU.mult)
+                    nc.sync.dma_start(dst, res[:])
+                else:
+                    nc.scalar.activation(res[:], acc[:], ACT.Copy, scale=-1.0 / S)
+                    (nc.scalar if h == 1 else nc.sync).dma_start(dst, res[:])

@@ -20,8 +20,8 @@ P = 128
 PACK = 4
 HALF = S // 2
 M_HALF = P // 2
-M_VECTOR = 44
-Z_VECTOR = 64
+M_VECTOR = 36
+PIECE = 128
 
 
 def tile_picked_deepset_relu_p_kernel(tc, x_words, x_scales, w1, w2_words, w2_scales, offs, out):
@@ -37,13 +37,26 @@ def tile_picked_deepset_relu_p_kernel(tc, x_words, x_scales, w1, w2_words, w2_sc
         offsets = tile("offsets", [P, S // 16], U16)
         xs_all = tile("xs_all", [P, T], U8)
         nc.vector.memset(xs_all[:].bitcast(I32), 0)
-        blank = shared.tile([P, 32], F32, name="blank", align_bytes=64, offset=4 * T - 64)
-        nc.vector.memset(blank[:], 0.0)
         xw_all = shared.tile([P, T], U32, name="xw_all", align_bytes=64, offset=0)
-        seed = tile("seed", [P, 32], F32)
-        seed_out = tile("seed_out", [P, 1], F32)
 
-        nc.vector.tensor_copy(seed[:], blank[:])
+
+        idle_bf = shared.tile([P, PACK * P], BF16, name="idle_bf", align_bytes=64, offset=4 * T - PACK * P)
+        idle_w = tile("idle_w", [P, P], U32)
+        idle_s = tile("idle_s", [P, P], U8)
+        nc.gpsimd.memset(idle_bf[:].bitcast(I32), 0)
+        nc.vector.quantize_mx(idle_w[:].bitcast(FP8X4), idle_s[:], idle_bf[:])
+
+        def keep_busy(bank, passes):
+            for n in range(passes):
+                nc.tensor.matmul_mx(
+                    bank[0:32, P * (n % 4) : P * (n % 4 + 1)],
+                    lhsT=idle_w[:, 0:32].bitcast(FP8X4),
+                    lhsT_scale=idle_s[:, 0:32],
+                    rhs=idle_w[:].bitcast(FP8X4),
+                    rhs_scale=xs[:, 0:P],
+                    start=True,
+                    stop=True,
+                )
 
         w1_rows = w1.rearrange("(p j) c -> p j c", j=PACK)
         w1_raw = [
@@ -55,33 +68,29 @@ def tile_picked_deepset_relu_p_kernel(tc, x_words, x_scales, w1, w2_words, w2_sc
         nc.sync.dma_start(offsets[:], offs)
         for q in range(4):
             nc.sync.dma_start(xs_all[32 * q : 32 * q + 4, :].bitcast(I32), x_scales[0, 4 * q : 4 * q + 4, :].bitcast(I32))
-        nc.scalar.activation(seed_out[:], seed[:, 0:1], ACT.Relu)
         nc.sync.dma_start(w1_raw[1][:], w1_rows[:, :, 256:512])
         nc.sync.dma_start(xw_all[:].bitcast(I32), x_words[0].rearrange("p n t -> p (n t)").bitcast(I32))
 
         xs = tile("xs", [P, S], U8)
         nc.vector.tensor_copy(xs[:], xs_all[:].indirect(offsets[:]))
 
-        w1_bf = [tile("w1_bf%d" % h, [P, PACK, M_HALF, PACK], BF16) for h in range(2)]
+        w1_bf = tile("w1_bf", [P, PACK, P, PACK], BF16)
 
-        def deal(copy, raw, raw_m0, half, m0, m1):
-            src = raw[:].rearrange("p j (m t) -> p m j t", t=PACK)[:, raw_m0 : raw_m0 + m1 - m0]
-            dst = w1_bf[half][:].rearrange("p t m j -> p m j t")[:, m0:m1]
+        def deal(copy, half, m0, m1):
+            src = w1_raw[half][:].rearrange("p j (m t) -> p m j t", t=PACK)[:, m0:m1]
+            dst = w1_bf[:].rearrange("p t m j -> p m j t")[:, M_HALF * half + m0 : M_HALF * half + m1]
             copy(dst, src)
+
+        def scalar_copy(dst, src):
+            nc.scalar.activation(dst, src, ACT.Copy)
+
+        deal(scalar_copy, 0, 0, M_HALF)
+        deal(nc.vector.tensor_copy, 1, 0, M_VECTOR)
+        deal(scalar_copy, 1, M_VECTOR, M_HALF)
 
         w1w = tile("w1w", [P, H], U32)
         w1s = tile("w1s", [P, H], U8)
-
-        def quantize_w1(half):
-            for t in range(PACK):
-                cols = slice(P * t + M_HALF * half, P * t + M_HALF * (half + 1))
-                nc.vector.quantize_mx(w1w[:, cols].bitcast(FP8X4), w1s[:, cols], w1_bf[half][:, t].rearrange("p m j -> p (m j)"))
-
-        deal(nc.scalar.copy, w1_raw[0], 0, 0, 0, M_HALF)
-        deal(nc.vector.tensor_copy, w1_raw[1], 0, 1, 0, M_VECTOR)
-        quantize_w1(0)
-        deal(nc.scalar.copy, w1_raw[1], M_VECTOR, 1, M_VECTOR, M_HALF)
-        quantize_w1(1)
+        nc.vector.quantize_mx(w1w[:].bitcast(FP8X4), w1s[:], w1_bf[:].rearrange("p t m j -> p (t m j)"))
 
         w2w = shared.tile([P, 2 * N], U8, name="w2w", align_bytes=64, offset=4 * T)
         nc.sync.dma_start(w2w[:].bitcast(I32), w2_words[0].bitcast(I32))
@@ -94,11 +103,15 @@ def tile_picked_deepset_relu_p_kernel(tc, x_words, x_scales, w1, w2_words, w2_sc
         for h in range(2):
             nc.vector.tensor_copy(xw[h][:], xw_all[:].indirect(offsets[:, 16 * h : 16 * (h + 1)]))
 
-        pre = [ps.tile([P, S], F32, name="pre%d" % t) for t in range(PACK)]
+        early = ps.tile([P, S], F32, name="early", tag="bank7")
+        keep_busy(early, 16)
+
+        split = [[ps.tile([P, HALF], F32, name="split%d%d" % (t, h), tag="bank%d" % (2 * t + h)) for h in range(2)] for t in range(2)]
+        whole = [ps.tile([P, S], F32, name="whole%d" % t, tag="bank%d" % (2 + t)) for t in (2, 3)]
 
         def layer1(t, h):
             nc.tensor.matmul_mx(
-                pre[t][:, HALF * h : HALF * (h + 1)],
+                split[t][h][:] if t < 2 else whole[t - 2][:, HALF * h : HALF * (h + 1)],
                 lhsT=w1w[:, P * t : P * (t + 1)].bitcast(FP8X4),
                 lhsT_scale=w1s[:, P * t : P * (t + 1)],
                 rhs=xw[h][:].bitcast(FP8X4),
@@ -107,53 +120,54 @@ def tile_picked_deepset_relu_p_kernel(tc, x_words, x_scales, w1, w2_words, w2_sc
                 stop=True,
             )
 
-        for t, h in ((0, 0), (1, 0), (0, 1), (1, 1), (2, 0), (2, 1), (3, 0), (3, 1)):
-            layer1(t, h)
+        for t in (0, 1, 2, 3):
+            layer1(t, 0)
+        for t in (2, 0, 3, 1):
+            layer1(t, 1)
 
         hid = [tile("hid%d" % t, [P, S], F32) for t in range(PACK)]
+        part = [tile("part%d" % t, [P, 1], F32) for t in range(2)]
         total = [tile("total%d" % t, [P, 1], F32) for t in range(PACK)]
         zt = tile("zt", [P, PACK, S], BF16)
-        for t in range(PACK):
-            if t == 1:
-                nc.vector.tensor_scalar(hid[t][:], pre[t][:], 0.0, None, ALU.max, ALU.add, accum_out=total[t][:])
-            else:
-                nc.scalar.activation(hid[t][:], pre[t][:], ACT.Relu, accum_out=total[t][:])
-        for t in range(PACK):
+        for t in (0, 1):
+            nc.scalar.activation(hid[t][:, :HALF], split[t][0][:], ACT.Relu, accum_out=part[t][:])
+        for t in (0, 1):
+            nc.scalar.activation(hid[t + 2][:], whole[t][:], ACT.Relu, accum_out=total[t + 2][:])
+            nc.vector.tensor_scalar(hid[t][:, HALF:], split[t][1][:], 0.0, part[t][:], ALU.max, ALU.add, accum_out=total[t][:])
+        late = ps.tile([P, S], F32, name="late", tag="bank5")
+        keep_busy(late, 8)
+        for t in (0, 2, 3):
             nc.vector.tensor_scalar(zt[:, t], hid[t][:], -float(S), total[t][:], ALU.mult, ALU.add)
+        nc.scalar.activation(zt[:, 1], hid[1][:], ACT.Identity, bias=total[1][:], scale=-float(S))
 
-        zi = [tile("zi%d" % h, [P, HALF, PACK], BF16) for h in range(2)]
+        pieces = range(S // PIECE)
+        zi = [tile("zi%d" % n, [P, PIECE, PACK], BF16) for n in pieces]
+        for n in pieces:
+            src = zt[:, :, PIECE * n : PIECE * (n + 1)].rearrange("p t (c i) -> p c t i", i=4)
+            dst = zi[n][:].rearrange("p (c i) t -> p c t i", i=4)
+            (nc.vector.tensor_copy if n < 2 else nc.scalar.copy)(dst, src)
 
-        def weave(copy, h, c0, c1):
-            src = zt[:, :, HALF * h + c0 : HALF * h + c1].rearrange("p t (c i) -> p c t i", i=4)
-            dst = zi[h][:, c0:c1].rearrange("p (c i) t -> p c t i", i=4)
-            copy(dst, src)
+        zw = [tile("zw%d" % n, [P, PIECE], U32) for n in pieces]
+        zs = [tile("zs%d" % n, [P, PIECE], U8) for n in pieces]
+        for n in pieces:
+            nc.vector.quantize_mx(zw[n][:].bitcast(FP8X4), zs[n][:], zi[n][:].rearrange("p c t -> p (c t)"))
 
-        weave(nc.vector.tensor_copy, 0, 0, HALF)
-        weave(nc.vector.tensor_copy, 1, 0, Z_VECTOR)
-        weave(nc.scalar.copy, 1, Z_VECTOR, HALF)
-
-        zw = [tile("zw%d" % h, [P, HALF], U32) for h in range(2)]
-        zs = [tile("zs%d" % h, [P, HALF], U8) for h in range(2)]
-        for h in range(2):
-            nc.vector.quantize_mx(zw[h][:].bitcast(FP8X4), zs[h][:], zi[h][:].rearrange("p c t -> p (c t)"))
-
-        for h in range(2):
+        out_rows = out.rearrange("(r p) c -> p r c", p=P)
+        for n in pieces:
+            acc = ps.tile([P, N // P, PIECE], F32, name="acc%d" % n, tag="bank%d" % ((6, 7, 0, 1)[n]))
             for r in range(N // P):
-                acc = ps.tile([P, HALF], F32, name="acc%d%d" % (h, r))
                 nc.tensor.matmul_mx(
-                    acc[:],
+                    acc[:, r],
                     lhsT=w2w[:, 2 * P * r : 2 * P * (r + 1)].bitcast(FP4X4),
                     lhsT_scale=w2s[:, P * r : P * (r + 1)],
-                    rhs=zw[h][:].bitcast(FP8X4),
-                    rhs_scale=zs[h][:],
+                    rhs=zw[n][:].bitcast(FP8X4),
+                    rhs_scale=zs[n][:],
                     start=True,
                     stop=True,
                 )
-                res = tile("res%d%d" % (h, r), [P, HALF], F32)
-                dst = out[P * r : P * (r + 1), HALF * h : HALF * (h + 1)]
-                if (h, r) == (1, 0):
-                    nc.vector.tensor_scalar(res[:], acc[:], -1.0 / S, None, ALU.mult)
-                    nc.sync.dma_start(dst, res[:])
-                else:
-                    nc.scalar.activation(res[:], acc[:], ACT.Copy, scale=-1.0 / S)
-                    (nc.scalar if h == 1 else nc.sync).dma_start(dst, res[:])
+            res = tile("res%d" % n, [P, N // P, PIECE], F32)
+            if n % 2:
+                nc.vector.tensor_scalar(res[:], acc[:], -1.0 / S, None, ALU.mult)
+            else:
+                nc.scalar.activation(res[:], acc[:], ACT.Copy, scale=-1.0 / S)
+            nc.sync.dma_start(out_rows[:, :, PIECE * n : PIECE * (n + 1)], res[:])

@@ -18,10 +18,15 @@ ACT = mybir.ActivationFunctionType
 
 P = 128
 PACK = 4
+QUADRANTS = 4
+PER_COLUMN = 16
 HALF = S // 2
 M_HALF = P // 2
 M_VECTOR = 36
 PIECE = 128
+RUN = 4
+WARM_COLUMNS = 32
+WARM_BEFORE, WARM_BETWEEN = 15, 9
 
 
 def tile_picked_deepset_relu_p_kernel(tc, x_words, x_scales, w1, w2_words, w2_scales, offs, out):
@@ -30,49 +35,57 @@ def tile_picked_deepset_relu_p_kernel(tc, x_words, x_scales, w1, w2_words, w2_sc
         sb = ctx.enter_context(tc.tile_pool(name="sb", bufs=1))
         shared = ctx.enter_context(tc.tile_pool(name="shared", bufs=1))
         ps = ctx.enter_context(tc.psum_pool(name="ps", bufs=1))
+        after_words = 4 * T
 
         def tile(name, shape, dtype):
             return sb.tile(shape, dtype, name=name, align_bytes=64)
 
-        offsets = tile("offsets", [P, S // 16], U16)
+        def placed(name, shape, dtype, offset):
+            return shared.tile(shape, dtype, name=name, align_bytes=64, offset=offset)
+
+        def bank(name, shape, number):
+            return ps.tile(shape, F32, name=name, tag="bank%d" % number)
+
+        def load_scale_rows(dst, src):
+            for q in range(QUADRANTS):
+                nc.sync.dma_start(dst[32 * q : 32 * q + 4, :].bitcast(I32), src[0, 4 * q : 4 * q + 4, :].bitcast(I32))
+
+        offsets = tile("offsets", [P, S // PER_COLUMN], U16)
         xs_all = tile("xs_all", [P, T], U8)
         nc.vector.memset(xs_all[:].bitcast(I32), 0)
-        xw_all = shared.tile([P, T], U32, name="xw_all", align_bytes=64, offset=0)
+        xw_all = placed("xw_all", [P, T], U32, 0)
 
-
-        idle_bf = shared.tile([P, PACK * P], BF16, name="idle_bf", align_bytes=64, offset=4 * T - PACK * P)
-        idle_w = tile("idle_w", [P, P], U32)
-        idle_s = tile("idle_s", [P, P], U8)
-        nc.gpsimd.memset(idle_bf[:].bitcast(I32), 0)
-        nc.vector.quantize_mx(idle_w[:].bitcast(FP8X4), idle_s[:], idle_bf[:])
-
-        def keep_busy(bank, passes):
-            for n in range(passes):
-                nc.tensor.matmul_mx(
-                    bank[0:32, P * (n % 4) : P * (n % 4 + 1)],
-                    lhsT=idle_w[:, 0:32].bitcast(FP8X4),
-                    lhsT_scale=idle_s[:, 0:32],
-                    rhs=idle_w[:].bitcast(FP8X4),
-                    rhs_scale=xs[:, 0:P],
-                    start=True,
-                    stop=True,
-                )
+        warm_bf = placed("warm_bf", [P, PACK * P], BF16, after_words - PACK * P)
+        warm_w = tile("warm_w", [P, P], U32)
+        warm_s = tile("warm_s", [P, P], U8)
+        nc.gpsimd.memset(warm_bf[:].bitcast(I32), 0)
+        nc.vector.quantize_mx(warm_w[:].bitcast(FP8X4), warm_s[:], warm_bf[:])
 
         w1_rows = w1.rearrange("(p j) c -> p j c", j=PACK)
-        w1_raw = [
-            tile("w1_raw0", [P, PACK, H // 2], F32),
-            shared.tile([P, PACK, H // 2], F32, name="w1_raw1", align_bytes=64, offset=4 * T),
-        ]
+        w1_raw = [tile("w1_raw0", [P, PACK, H // 2], F32), placed("w1_raw1", [P, PACK, H // 2], F32, after_words)]
 
-        nc.sync.dma_start(w1_raw[0][:], w1_rows[:, :, 0:256])
+        nc.sync.dma_start(w1_raw[0][:], w1_rows[:, :, : H // 2])
         nc.sync.dma_start(offsets[:], offs)
-        for q in range(4):
-            nc.sync.dma_start(xs_all[32 * q : 32 * q + 4, :].bitcast(I32), x_scales[0, 4 * q : 4 * q + 4, :].bitcast(I32))
-        nc.sync.dma_start(w1_raw[1][:], w1_rows[:, :, 256:512])
+        load_scale_rows(xs_all, x_scales)
+        nc.sync.dma_start(w1_raw[1][:], w1_rows[:, :, H // 2 :])
         nc.sync.dma_start(xw_all[:].bitcast(I32), x_words[0].rearrange("p n t -> p (n t)").bitcast(I32))
 
         xs = tile("xs", [P, S], U8)
-        nc.vector.tensor_copy(xs[:], xs_all[:].indirect(offsets[:]))
+        nc.vector.tensor_copy(xs[:, :P], xs_all[:].indirect(offsets[:, : P // PER_COLUMN]))
+        nc.vector.tensor_copy(xs[:, P:], xs_all[:].indirect(offsets[:, P // PER_COLUMN :]))
+
+        def warm_up(scratch, passes):
+            for n in range(passes):
+                slot = n % (S // P)
+                nc.tensor.matmul_mx(
+                    scratch[:WARM_COLUMNS, P * slot : P * (slot + 1)],
+                    lhsT=warm_w[:, :WARM_COLUMNS].bitcast(FP8X4),
+                    lhsT_scale=warm_s[:, :WARM_COLUMNS],
+                    rhs=warm_w[:].bitcast(FP8X4),
+                    rhs_scale=xs[:, :P],
+                    start=True,
+                    stop=True,
+                )
 
         w1_bf = tile("w1_bf", [P, PACK, P, PACK], BF16)
 
@@ -81,37 +94,36 @@ def tile_picked_deepset_relu_p_kernel(tc, x_words, x_scales, w1, w2_words, w2_sc
             dst = w1_bf[:].rearrange("p t m j -> p m j t")[:, M_HALF * half + m0 : M_HALF * half + m1]
             copy(dst, src)
 
-        def scalar_copy(dst, src):
+        def round_on_scalar(dst, src):
             nc.scalar.activation(dst, src, ACT.Copy)
 
-        deal(scalar_copy, 0, 0, M_HALF)
+        deal(round_on_scalar, 0, 0, M_HALF)
         deal(nc.vector.tensor_copy, 1, 0, M_VECTOR)
-        deal(scalar_copy, 1, M_VECTOR, M_HALF)
+        deal(round_on_scalar, 1, M_VECTOR, M_HALF)
 
         w1w = tile("w1w", [P, H], U32)
         w1s = tile("w1s", [P, H], U8)
         nc.vector.quantize_mx(w1w[:].bitcast(FP8X4), w1s[:], w1_bf[:].rearrange("p t m j -> p (t m j)"))
 
-        w2w = shared.tile([P, 2 * N], U8, name="w2w", align_bytes=64, offset=4 * T)
+        w2w = placed("w2w", [P, 2 * N], U8, after_words)
         nc.sync.dma_start(w2w[:].bitcast(I32), w2_words[0].bitcast(I32))
-
-        w2s = shared.tile([P, N], U8, name="w2s", align_bytes=64, offset=4 * T + 2 * N)
+        w2s = placed("w2s", [P, N], U8, after_words + 2 * N)
         nc.gpsimd.memset(w2s[:].bitcast(I32), 0)
-        for q in range(4):
-            nc.sync.dma_start(w2s[32 * q : 32 * q + 4, :].bitcast(I32), w2_scales[0, 4 * q : 4 * q + 4, :].bitcast(I32))
+        load_scale_rows(w2s, w2_scales)
+
         xw = [tile("xw%d" % h, [P, HALF], U32) for h in range(2)]
+        columns = HALF // PER_COLUMN
         for h in range(2):
-            nc.vector.tensor_copy(xw[h][:], xw_all[:].indirect(offsets[:, 16 * h : 16 * (h + 1)]))
+            nc.vector.tensor_copy(xw[h][:], xw_all[:].indirect(offsets[:, columns * h : columns * (h + 1)]))
 
-        early = ps.tile([P, S], F32, name="early", tag="bank7")
-        keep_busy(early, 16)
+        warm_up(bank("warm_before", [P, S], 7), WARM_BEFORE)
 
-        split = [[ps.tile([P, HALF], F32, name="split%d%d" % (t, h), tag="bank%d" % (2 * t + h)) for h in range(2)] for t in range(2)]
-        whole = [ps.tile([P, S], F32, name="whole%d" % t, tag="bank%d" % (2 + t)) for t in (2, 3)]
+        split = [[bank("split%d%d" % (t, h), [P, HALF], 2 * t + h) for h in range(2)] for t in range(2)]
+        whole = {t: bank("whole%d" % t, [P, S], 2 + t) for t in (2, 3)}
 
         def layer1(t, h):
             nc.tensor.matmul_mx(
-                split[t][h][:] if t < 2 else whole[t - 2][:, HALF * h : HALF * (h + 1)],
+                whole[t][:, HALF * h : HALF * (h + 1)] if t in whole else split[t][h][:],
                 lhsT=w1w[:, P * t : P * (t + 1)].bitcast(FP8X4),
                 lhsT_scale=w1s[:, P * t : P * (t + 1)],
                 rhs=xw[h][:].bitcast(FP8X4),
@@ -120,54 +132,90 @@ def tile_picked_deepset_relu_p_kernel(tc, x_words, x_scales, w1, w2_words, w2_sc
                 stop=True,
             )
 
-        for t in (0, 1, 2, 3):
+        for t in range(PACK):
             layer1(t, 0)
-        for t in (2, 0, 3, 1):
+        for t in range(2):
+            layer1(t + 2, 1)
             layer1(t, 1)
 
         hid = [tile("hid%d" % t, [P, S], F32) for t in range(PACK)]
         part = [tile("part%d" % t, [P, 1], F32) for t in range(2)]
         total = [tile("total%d" % t, [P, 1], F32) for t in range(PACK)]
         zt = tile("zt", [P, PACK, S], BF16)
-        for t in (0, 1):
+        for t in range(2):
             nc.scalar.activation(hid[t][:, :HALF], split[t][0][:], ACT.Relu, accum_out=part[t][:])
-        for t in (0, 1):
-            nc.scalar.activation(hid[t + 2][:], whole[t][:], ACT.Relu, accum_out=total[t + 2][:])
+        for t in range(2):
+            nc.scalar.activation(hid[t + 2][:], whole[t + 2][:], ACT.Relu, accum_out=total[t + 2][:])
             nc.vector.tensor_scalar(hid[t][:, HALF:], split[t][1][:], 0.0, part[t][:], ALU.max, ALU.add, accum_out=total[t][:])
-        late = ps.tile([P, S], F32, name="late", tag="bank5")
-        keep_busy(late, 8)
-        for t in (0, 2, 3):
-            nc.vector.tensor_scalar(zt[:, t], hid[t][:], -float(S), total[t][:], ALU.mult, ALU.add)
-        nc.scalar.activation(zt[:, 1], hid[1][:], ACT.Identity, bias=total[1][:], scale=-float(S))
+
+        warm_up(bank("warm_between", [P, S], 5), WARM_BETWEEN)
+
+        def centre_on_vector(t, cols):
+            nc.vector.tensor_scalar(zt[:, t, cols], hid[t][:, cols], -float(S), total[t][:], ALU.mult, ALU.add)
+
+        def centre_on_scalar(t, cols):
+            nc.scalar.activation(zt[:, t, cols], hid[t][:, cols], ACT.Identity, bias=total[t][:], scale=-float(S))
+
+        centre_on_vector(0, slice(0, S))
+        centre_on_vector(2, slice(0, S))
+        for cols in (slice(0, PIECE), slice(PIECE, S)):
+            centre_on_vector(3, cols)
+            centre_on_scalar(1, cols)
 
         pieces = range(S // PIECE)
+        last = pieces[-1]
         zi = [tile("zi%d" % n, [P, PIECE, PACK], BF16) for n in pieces]
-        for n in pieces:
-            src = zt[:, :, PIECE * n : PIECE * (n + 1)].rearrange("p t (c i) -> p c t i", i=4)
-            dst = zi[n][:].rearrange("p (c i) t -> p c t i", i=4)
-            (nc.vector.tensor_copy if n < 2 else nc.scalar.copy)(dst, src)
-
         zw = [tile("zw%d" % n, [P, PIECE], U32) for n in pieces]
         zs = [tile("zs%d" % n, [P, PIECE], U8) for n in pieces]
-        for n in pieces:
+
+        def interleave(copy, n, c0, c1):
+            src = zt[:, :, PIECE * n + c0 : PIECE * n + c1].rearrange("p t (c i) -> p c t i", i=RUN)
+            dst = zi[n][:, c0:c1].rearrange("p (c i) t -> p c t i", i=RUN)
+            copy(dst, src)
+
+        def quantize_z(n):
             nc.vector.quantize_mx(zw[n][:].bitcast(FP8X4), zs[n][:], zi[n][:].rearrange("p c t -> p (c t)"))
 
+        interleave(nc.vector.tensor_copy, 0, 0, PIECE)
+        interleave(nc.vector.tensor_copy, 1, 0, PIECE)
+        interleave(nc.scalar.copy, 2, 0, PIECE)
+        interleave(nc.scalar.copy, 3, 0, PIECE // 2)
+        quantize_z(0)
+        quantize_z(1)
+        interleave(nc.vector.tensor_copy, 3, PIECE // 2, PIECE)
+        quantize_z(2)
+        quantize_z(3)
+
+        def layer2(acc, r, n):
+            nc.tensor.matmul_mx(
+                acc,
+                lhsT=w2w[:, 2 * P * r : 2 * P * (r + 1)].bitcast(FP4X4),
+                lhsT_scale=w2s[:, P * r : P * (r + 1)],
+                rhs=zw[n][:].bitcast(FP8X4),
+                rhs_scale=zs[n][:],
+                start=True,
+                stop=True,
+            )
+
+        def leave_on_vector(dst, acc):
+            nc.vector.tensor_scalar(dst, acc, -1.0 / S, None, ALU.mult)
+
+        def leave_on_scalar(dst, acc):
+            nc.scalar.activation(dst, acc, ACT.Copy, scale=-1.0 / S)
+
+        piece_bank = (6, 7, 0)
+        last_bank = (1, 2)
         out_rows = out.rearrange("(r p) c -> p r c", p=P)
         for n in pieces:
-            acc = ps.tile([P, N // P, PIECE], F32, name="acc%d" % n, tag="bank%d" % ((6, 7, 0, 1)[n]))
-            for r in range(N // P):
-                nc.tensor.matmul_mx(
-                    acc[:, r],
-                    lhsT=w2w[:, 2 * P * r : 2 * P * (r + 1)].bitcast(FP4X4),
-                    lhsT_scale=w2s[:, P * r : P * (r + 1)],
-                    rhs=zw[n][:].bitcast(FP8X4),
-                    rhs_scale=zs[n][:],
-                    start=True,
-                    stop=True,
-                )
             res = tile("res%d" % n, [P, N // P, PIECE], F32)
-            if n % 2:
-                nc.vector.tensor_scalar(res[:], acc[:], -1.0 / S, None, ALU.mult)
+            if n == last:
+                for r, leave in enumerate((leave_on_vector, leave_on_scalar)):
+                    acc = bank("acc_last%d" % r, [P, PIECE], last_bank[r])
+                    layer2(acc[:], r, n)
+                    leave(res[:, r], acc[:])
             else:
-                nc.scalar.activation(res[:], acc[:], ACT.Copy, scale=-1.0 / S)
+                acc = bank("acc%d" % n, [P, N // P, PIECE], piece_bank[n])
+                for r in range(N // P):
+                    layer2(acc[:, r], r, n)
+                (leave_on_vector if n % 2 else leave_on_scalar)(res[:], acc[:])
             nc.sync.dma_start(out_rows[:, :, PIECE * n : PIECE * (n + 1)], res[:])

from contextlib import ExitStack

import concourse.mybir as mybir

K, T, S, H, N = 512, 1024, 512, 512, 256
FLOPS = 2 * K * H * S + 2 * H * N * S

F32 = mybir.dt.float32
BF16 = mybir.dt.bfloat16
I32 = mybir.dt.int32
U32 = mybir.dt.uint32
U16 = mybir.dt.uint16
U8 = mybir.dt.uint8
FP8X4 = mybir.dt.float8_e4m3fn_x4
FP4X4 = mybir.dt.float4_e2m1fn_x4
ALU = mybir.AluOpType
ACT = mybir.ActivationFunctionType

P = 128
PACK = 4
QUADRANTS = 4
PER_COLUMN = 16
HALF = S // 2
M_HALF = P // 2
M_VECTOR = 36
PIECE = 128
RUN = 4
WARM_COLUMNS = 32
WARM_BEFORE, WARM_BETWEEN = 15, 9


def tile_picked_deepset_relu_p_kernel(tc, x_words, x_scales, w1, w2_words, w2_scales, offs, out):
    nc = tc.nc
    with ExitStack() as ctx:
        sb = ctx.enter_context(tc.tile_pool(name="sb", bufs=1))
        shared = ctx.enter_context(tc.tile_pool(name="shared", bufs=1))
        ps = ctx.enter_context(tc.psum_pool(name="ps", bufs=1))
        after_words = 4 * T

        def tile(name, shape, dtype):
            return sb.tile(shape, dtype, name=name, align_bytes=64)

        def placed(name, shape, dtype, offset):
            return shared.tile(shape, dtype, name=name, align_bytes=64, offset=offset)

        def bank(name, shape, number):
            return ps.tile(shape, F32, name=name, tag="bank%d" % number)

        def load_scale_rows(dst, src):
            for q in range(QUADRANTS):
                nc.sync.dma_start(dst[32 * q : 32 * q + 4, :].bitcast(I32), src[0, 4 * q : 4 * q + 4, :].bitcast(I32))

        offsets = tile("offsets", [P, S // PER_COLUMN], U16)
        xs_all = tile("xs_all", [P, T], U8)
        nc.vector.memset(xs_all[:].bitcast(I32), 0)
        xw_all = placed("xw_all", [P, T], U32, 0)

        warm_bf = placed("warm_bf", [P, PACK * P], BF16, after_words - PACK * P)
        warm_w = tile("warm_w", [P, P], U32)
        warm_s = tile("warm_s", [P, P], U8)
        nc.gpsimd.memset(warm_bf[:].bitcast(I32), 0)
        nc.vector.quantize_mx(warm_w[:].bitcast(FP8X4), warm_s[:], warm_bf[:])

        w1_rows = w1.rearrange("(p j) c -> p j c", j=PACK)
        w1_raw = [tile("w1_raw0", [P, PACK, H // 2], F32), placed("w1_raw1", [P, PACK, H // 2], F32, after_words)]

        nc.sync.dma_start(w1_raw[0][:], w1_rows[:, :, : H // 2])
        nc.sync.dma_start(offsets[:], offs)
        load_scale_rows(xs_all, x_scales)
        nc.sync.dma_start(w1_raw[1][:], w1_rows[:, :, H // 2 :])
        nc.sync.dma_start(xw_all[:].bitcast(I32), x_words[0].rearrange("p n t -> p (n t)").bitcast(I32))

        xs = tile("xs", [P, S], U8)
        nc.vector.tensor_copy(xs[:, :P], xs_all[:].indirect(offsets[:, : P // PER_COLUMN]))
        nc.vector.tensor_copy(xs[:, P:], xs_all[:].indirect(offsets[:, P // PER_COLUMN :]))

        def warm_up(scratch, passes):
            for n in range(passes):
                slot = n % (S // P)
                nc.tensor.matmul_mx(
                    scratch[:WARM_COLUMNS, P * slot : P * (slot + 1)],
                    lhsT=warm_w[:, :WARM_COLUMNS].bitcast(FP8X4),
                    lhsT_scale=warm_s[:, :WARM_COLUMNS],
                    rhs=warm_w[:].bitcast(FP8X4),
                    rhs_scale=xs[:, :P],
                    start=True,
                    stop=True,
                )

        w1_bf = tile("w1_bf", [P, PACK, P, PACK], BF16)

        def deal(copy, half, m0, m1):
            src = w1_raw[half][:].rearrange("p j (m t) -> p m j t", t=PACK)[:, m0:m1]
            dst = w1_bf[:].rearrange("p t m j -> p m j t")[:, M_HALF * half + m0 : M_HALF * half + m1]
            copy(dst, src)

        def round_on_scalar(dst, src):
            nc.scalar.activation(dst, src, ACT.Copy)

        deal(round_on_scalar, 0, 0, M_HALF)
        deal(nc.vector.tensor_copy, 1, 0, M_VECTOR)
        deal(round_on_scalar, 1, M_VECTOR, M_HALF)

        w1w = tile("w1w", [P, H], U32)
        w1s = tile("w1s", [P, H], U8)
        nc.vector.quantize_mx(w1w[:].bitcast(FP8X4), w1s[:], w1_bf[:].rearrange("p t m j -> p (t m j)"))

        w2w = placed("w2w", [P, 2 * N], U8, after_words)
        nc.sync.dma_start(w2w[:].bitcast(I32), w2_words[0].bitcast(I32))
        w2s = placed("w2s", [P, N], U8, after_words + 2 * N)
        nc.gpsimd.memset(w2s[:].bitcast(I32), 0)
        load_scale_rows(w2s, w2_scales)

        xw = [tile("xw%d" % h, [P, HALF], U32) for h in range(2)]
        columns = HALF // PER_COLUMN
        for h in range(2):
            nc.vector.tensor_copy(xw[h][:], xw_all[:].indirect(offsets[:, columns * h : columns * (h + 1)]))

        warm_up(bank("warm_before", [P, S], 7), WARM_BEFORE)

        split = [[bank("split%d%d" % (t, h), [P, HALF], 2 * t + h) for h in range(2)] for t in range(2)]
        whole = {t: bank("whole%d" % t, [P, S], 2 + t) for t in (2, 3)}

        def layer1(t, h):
            nc.tensor.matmul_mx(
                whole[t][:, HALF * h : HALF * (h + 1)] if t in whole else split[t][h][:],
                lhsT=w1w[:, P * t : P * (t + 1)].bitcast(FP8X4),
                lhsT_scale=w1s[:, P * t : P * (t + 1)],
                rhs=xw[h][:].bitcast(FP8X4),
                rhs_scale=xs[:, HALF * h : HALF * (h + 1)],
                start=True,
                stop=True,
            )

        for t in range(PACK):
            layer1(t, 0)
        for t in range(2):
            layer1(t + 2, 1)
            layer1(t, 1)

        hid = [tile("hid%d" % t, [P, S], F32) for t in range(PACK)]
        part = [tile("part%d" % t, [P, 1], F32) for t in range(2)]
        total = [tile("total%d" % t, [P, 1], F32) for t in range(PACK)]
        zt = tile("zt", [P, PACK, S], BF16)
        for t in range(2):
            nc.scalar.activation(hid[t][:, :HALF], split[t][0][:], ACT.Relu, accum_out=part[t][:])
        for t in range(2):
            nc.scalar.activation(hid[t + 2][:], whole[t + 2][:], ACT.Relu, accum_out=total[t + 2][:])
            nc.vector.tensor_scalar(hid[t][:, HALF:], split[t][1][:], 0.0, part[t][:], ALU.max, ALU.add, accum_out=total[t][:])

        warm_up(bank("warm_between", [P, S], 5), WARM_BETWEEN)

        def centre_on_vector(t, cols):
            nc.vector.tensor_scalar(zt[:, t, cols], hid[t][:, cols], -float(S), total[t][:], ALU.mult, ALU.add)

        def centre_on_scalar(t, cols):
            nc.scalar.activation(zt[:, t, cols], hid[t][:, cols], ACT.Identity, bias=total[t][:], scale=-float(S))

        centre_on_vector(0, slice(0, S))
        centre_on_vector(2, slice(0, S))
        for cols in (slice(0, PIECE), slice(PIECE, S)):
            centre_on_vector(3, cols)
            centre_on_scalar(1, cols)

        pieces = range(S // PIECE)
        last = pieces[-1]
        zi = [tile("zi%d" % n, [P, PIECE, PACK], BF16) for n in pieces]
        zw = [tile("zw%d" % n, [P, PIECE], U32) for n in pieces]
        zs = [tile("zs%d" % n, [P, PIECE], U8) for n in pieces]

        def interleave(copy, n, c0, c1):
            src = zt[:, :, PIECE * n + c0 : PIECE * n + c1].rearrange("p t (c i) -> p c t i", i=RUN)
            dst = zi[n][:, c0:c1].rearrange("p (c i) t -> p c t i", i=RUN)
            copy(dst, src)

        def quantize_z(n):
            nc.vector.quantize_mx(zw[n][:].bitcast(FP8X4), zs[n][:], zi[n][:].rearrange("p c t -> p (c t)"))

        interleave(nc.vector.tensor_copy, 0, 0, PIECE)
        interleave(nc.vector.tensor_copy, 1, 0, PIECE)
        interleave(nc.scalar.copy, 2, 0, PIECE)
        interleave(nc.scalar.copy, 3, 0, PIECE // 2)
        quantize_z(0)
        quantize_z(1)
        interleave(nc.vector.tensor_copy, 3, PIECE // 2, PIECE)
        quantize_z(2)
        quantize_z(3)

        def layer2(acc, r, n):
            nc.tensor.matmul_mx(
                acc,
                lhsT=w2w[:, 2 * P * r : 2 * P * (r + 1)].bitcast(FP4X4),
                lhsT_scale=w2s[:, P * r : P * (r + 1)],
                rhs=zw[n][:].bitcast(FP8X4),
                rhs_scale=zs[n][:],
                start=True,
                stop=True,
            )

        def leave_on_vector(dst, acc):
            nc.vector.tensor_scalar(dst, acc, -1.0 / S, None, ALU.mult)

        def leave_on_scalar(dst, acc):
            nc.scalar.activation(dst, acc, ACT.Copy, scale=-1.0 / S)

        piece_bank = (6, 7, 0)
        last_bank = (1, 2)
        out_rows = out.rearrange("(r p) c -> p r c", p=P)
        for n in pieces:
            res = tile("res%d" % n, [P, N // P, PIECE], F32)
            if n == last:
                for r, leave in enumerate((leave_on_vector, leave_on_scalar)):
                    acc = bank("acc_last%d" % r, [P, PIECE], last_bank[r])
                    layer2(acc[:], r, n)
                    leave(res[:, r], acc[:])
            else:
                acc = bank("acc%d" % n, [P, N // P, PIECE], piece_bank[n])
                for r in range(N // P):
                    layer2(acc[:, r], r, n)
                (leave_on_vector if n % 2 else leave_on_scalar)(res[:], acc[:])
            nc.sync.dma_start(out_rows[:, :, PIECE * n : PIECE * (n + 1)], res[:])
